import numpy as np
import ml_dtypes


def mxq(x, axis, fmt="e4m3"):
    dtype, down = {"e4m3": (ml_dtypes.float8_e4m3fn, 7), "e5m2": (ml_dtypes.float8_e5m2, 14)}[fmt]
    v = np.moveaxis(np.asarray(x, np.float32).astype(ml_dtypes.bfloat16).astype(np.float64), axis, -1)
    blocks = v.reshape(v.shape[:-1] + (-1, 32))
    amax = np.abs(blocks).max(-1, keepdims=True)
    byte = np.maximum(np.where(amax > 0, np.frexp(amax)[1] - 1 + 127, 0) - down, 1)
    scale = np.exp2(byte - 127.0)
    codes = (blocks / scale).astype(np.float32).astype(dtype).astype(np.float64)
    return np.moveaxis((codes * scale).reshape(v.shape), -1, axis)


WIDE = False


def mx_kscale(k):
    if not WIDE:
        return np.ones(k)
    levels = np.array([10, -10, 5, -5, 0])
    if k % 512:
        return np.exp2(np.random.permutation(np.resize(levels, k // 32))).repeat(32)
    a = np.empty((k // 512, 16))
    for p in range(k // 512):
        a[p, :8] = np.random.permutation(np.resize(levels, 8))
        for g in range(8):
            far = levels[np.abs(levels - a[p, g]) >= 10]
            a[p, g + 8] = far[np.random.randint(len(far))]
    return np.exp2(a.ravel()).repeat(32)


def f64(x):
    return np.asarray(x).astype(np.float64)


def striped(idx):
    return np.tile(idx.reshape(-1, 16).T, (8, 1)).astype(np.uint16)


def unstriped(offs):
    return offs[:16].T.reshape(-1).astype(np.int64)


def pack_weight(w):
    k, n = w.shape
    w = f64(np.asarray(w, np.float32).astype(ml_dtypes.bfloat16)).reshape(k // 32, 32, n)
    amax = np.abs(w).max(1)
    byte = np.clip(np.where(amax > 0, np.frexp(amax)[1] - 1 + 127 - 7, 1), 1, 254)
    scaled = (w * np.exp2(127.0 - byte)[:, None, :]).reshape(k, n).astype(np.float32)
    words = np.ascontiguousarray(scaled.reshape(k // 512, 128, 4, n).transpose(0, 1, 3, 2)).astype(ml_dtypes.float8_e4m3fn).view(np.uint8)
    return words, np.ascontiguousarray(byte.astype(np.uint8).reshape(k // 512, 16, n))


def unpack_weight(words, scales):
    g, p, n, _ = words.shape
    vals = np.ascontiguousarray(words).view(ml_dtypes.float8_e4m3fn).astype(np.float64) * np.repeat(np.exp2(scales.astype(np.float64) - 127.0), 8, axis=1)[..., None]
    return vals.transpose(0, 1, 3, 2).reshape(g * 512, n)


E2M1 = np.array([0.0, 0.5, 1.0, 1.5, 2.0, 3.0, 4.0, 6.0, -0.0, -0.5, -1.0, -1.5, -2.0, -3.0, -4.0, -6.0])


def pack_fp4(w):
    k, n = w.shape
    w = f64(np.asarray(w, np.float32).astype(ml_dtypes.bfloat16)).reshape(k // 32, 32, n)
    amax = np.abs(w).max(1)
    mant, ex = np.frexp(amax / 6.0)
    byte = np.clip(np.where(amax > 0, np.where(mant > 0.5, ex, ex - 1) + 127, 1), 1, 254)
    scaled = (w * np.exp2(127.0 - byte)[:, None, :]).reshape(k, n).astype(np.float32)
    c = np.ascontiguousarray(scaled.reshape(k // 512, 128, 4, n).transpose(0, 1, 3, 2)).astype(ml_dtypes.float4_e2m1fn).view(np.uint8) & 0xF
    words = (c[..., 0::2] | (c[..., 1::2] << 4)).reshape(k // 512, 128, 2 * n)
    return np.ascontiguousarray(words), np.ascontiguousarray(byte.astype(np.uint8).reshape(k // 512, 16, n))


def unpack_fp4(words, scales):
    g, _, n = scales.shape
    words = np.ascontiguousarray(words).reshape(g, 128, n, 2)
    nib = np.empty((g, 128, n, 4), np.uint8)
    nib[..., 0::2] = words & 0xF
    nib[..., 1::2] = words >> 4
    vals = E2M1[nib] * np.repeat(np.exp2(scales.astype(np.float64) - 127.0), 8, axis=1)[..., None]
    return vals.transpose(0, 1, 3, 2).reshape(g * 512, n)


def sigmoid(v):
    return 1.0 / (1.0 + np.exp(-np.maximum(v, -700.0)))


K, T, S, N, H = 512, 1024, 512, 256, 512


def setup_inputs():
    n = np.random.standard_normal
    s = mx_kscale(K)[:, None]
    u = mx_kscale(H)
    packed_xT = pack_weight(n((K, T)) * s)
    packed_w1 = pack_fp4(n((K, H)) / np.sqrt(K) / s)
    packed_w2 = pack_fp4(n((K, H)) / np.sqrt(K) / s)
    packed_w3 = pack_fp4(n((H, N)) / np.sqrt(H) / u[:, None])
    return {
        "x_words": packed_xT[0],
        "x_scales": packed_xT[1],
        "w1_words": packed_w1[0],
        "w1_scales": packed_w1[1],
        "w2_words": packed_w2[0],
        "w2_scales": packed_w2[1],
        "aa": (np.random.uniform(0.1, 0.3, (H, S))).astype(np.float32),
        "unit": (np.random.uniform(0.6, 1.4, (H, 1)) * u[:, None]).astype(np.float32),
        "w3_words": packed_w3[0],
        "w3_scales": packed_w3[1],
        "offs": striped(np.random.permutation(T)[:S]),
        "shl": striped(np.random.permutation(S)),
    }


def reference(x_words, x_scales, w1_words, w1_scales, w2_words, w2_scales, aa, unit, w3_words, w3_scales, offs, shl):
    xq = unpack_weight(x_words, x_scales)[:, unstriped(offs)]
    rt = unpack_fp4(w2_words, w2_scales).T @ xq
    rs = rt[:, unstriped(shl)]
    vsh = sigmoid(rs - rt)
    po = unpack_fp4(w1_words, w1_scales).T @ xq
    por = 0.4 * sigmoid(po) + 0.05
    ff = f64(aa) / ((por) ** 2)
    cond = (-1.0 * vsh + 1.0) / ff + 0.5 * vsh
    res = np.log(np.exp(rt) + 1.0) + 0.2
    sw = np.sqrt(cond / (cond * res + 0.1) + 0.02)
    hid = f64(unit) * (sw * por - (0.3 * vsh[:, unstriped(shl)]))
    return unpack_fp4(w3_words, w3_scales).T @ mxq(hid, 0, "e4m3")

@@ -1,0 +1,215 @@
+import math
+from contextlib import ExitStack
+
+import concourse.mybir as mybir
+from concourse.masks import make_identity
+
+K, T, S, N, H = 512, 1024, 512, 256, 512
+FLOPS = 2 * K * S * H * 2 + 2 * H * S * N
+
+F32 = mybir.dt.float32
+BF16 = mybir.dt.bfloat16
+I32 = mybir.dt.int32
+U32 = mybir.dt.uint32
+U16 = mybir.dt.uint16
+U8 = mybir.dt.uint8
+FP8X4 = mybir.dt.float8_e4m3fn_x4
+FP4X4 = mybir.dt.float4_e2m1fn_x4
+ACT = mybir.ActivationFunctionType
+ALU = mybir.AluOpType
+
+P = 128
+RT = H // P
+NB = S // P
+MT = N // P
+HALF = S // 2
+TINY = 1e-14
+ON_VECTOR = 2
+
+
+def load_scales(nc, plane, scales):
+    for q in range(4):
+        nc.sync.dma_start(out=plane[32 * q : 32 * q + 4, :].bitcast(I32), in_=scales[0, 4 * q : 4 * q + 4, :].bitcast(I32))
+
+
+def tile_picked_yarchi_bvw_p_kernel(tc, x_words, x_scales, w1_words, w1_scales, w2_words, w2_scales, aa, unit, w3_words, w3_scales, offs, shl, out):
+    nc = tc.nc
+    with ExitStack() as ctx:
+        keep = ctx.enter_context(tc.tile_pool(name="keep", bufs=1))
+        psum = ctx.enter_context(tc.psum_pool(name="psum", bufs=1))
+
+        def bank(n):
+            return psum.tile([P, S], F32, name="bank%d" % n)
+
+        def wide(name):
+            return keep.tile([P, RT, S], F32, name=name, align_bytes=64)
+
+        def cols(b):
+            return slice(P * b, P * (b + 1))
+
+        offs_t = keep.tile([P, S // 16], U16, name="offs_t")
+        shl_t = keep.tile([P, S // 16], U16, name="shl_t")
+        xw = keep.tile([P, T], I32, name="xw", align_bytes=64)
+        xs = keep.tile([P, T], U8, name="xs", align_bytes=64)
+        w2w = keep.tile([P, 2 * H], U8, name="w2w", align_bytes=64)
+        w1w = keep.tile([P, 2 * H], U8, name="w1w", align_bytes=64)
+        w3w = keep.tile([P, 2 * N], U8, name="w3w", align_bytes=64)
+        w2s = keep.tile([P, H], U8, name="w2s", align_bytes=64)
+        w1s = keep.tile([P, H], U8, name="w1s", align_bytes=64)
+        w3s = keep.tile([P, N], U8, name="w3s", align_bytes=64)
+        ucol = keep.tile([P, 4], F32, name="ucol")
+        ident = keep.tile([P, P], F32, name="ident")
+        a_t = wide("a_t")
+
+        for plane in (xs, w2s):
+            nc.vector.memset(plane[:].bitcast(I32), 0)
+        for plane in (w1s, w3s):
+            nc.vector.memset(plane[:].bitcast(I32), 0)
+        win = [keep.tile([P, S + 16], F32, name="win%d" % t, align_bytes=64) for t in range(RT)]
+        vb = [keep.tile([P, S + (192 if t < ON_VECTOR else 16)], F32, name="vb%d" % t, align_bytes=64) for t in range(RT)]
+        for window in win + vb:
+            nc.vector.memset(window[:, S:], 0.0)
+
+        a_v = aa.rearrange("(t p) j -> p t j", p=P)
+        nc.sync.dma_start(offs_t[:], offs)
+        load_scales(nc, xs, x_scales)
+        nc.sync.dma_start(out=xw[:], in_=x_words[0].rearrange("p n t -> p (n t)").bitcast(I32))
+        nc.sync.dma_start(out=a_t[:, 0:2, :], in_=a_v[:, 0:2, :])
+        nc.sync.dma_start(out=a_t[:, 2:4, :], in_=a_v[:, 2:4, :])
+        load_scales(nc, w2s, w2_scales)
+        nc.sync.dma_start(out=w2w[:].bitcast(I32), in_=w2_words[0].bitcast(I32))
+        nc.sync.dma_start(shl_t[:], shl)
+        nc.sync.dma_start(out=w1w[:].bitcast(I32), in_=w1_words[0].bitcast(I32))
+        load_scales(nc, w1s, w1_scales)
+        nc.gpsimd.dma_start(out=ucol[:], in_=unit.rearrange("(p t) o -> p (t o)", t=4))
+        nc.sync.dma_start(out=w3w[:].bitcast(I32), in_=w3_words[0].bitcast(I32))
+        load_scales(nc, w3s, w3_scales)
+        make_identity(nc, ident[:])
+
+        xg = keep.tile([P, S], U32, name="xg", align_bytes=64)
+        xsg = keep.tile([P, S], U8, name="xsg", align_bytes=64)
+        nc.vector.tensor_copy(xsg[:], xs[:].indirect(offs_t[:]))
+        for h in range(2):
+            nc.vector.tensor_copy(xg[:, HALF * h : HALF * (h + 1)], xw[:].bitcast(U32).indirect(offs_t[:, (HALF // 16) * h : (HALF // 16) * (h + 1)]))
+
+        def first_product(acc, words, plane, t, js):
+            nc.tensor.matmul_mx(
+                out=acc[:, js],
+                lhsT=words[:, 2 * P * t : 2 * P * (t + 1)].bitcast(FP4X4),
+                lhsT_scale=plane[:, cols(t)],
+                rhs=xg[:, js].bitcast(FP8X4),
+                rhs_scale=xsg[:, js],
+                start=True,
+                stop=True,
+            )
+
+        ub_ps = bank(4)
+        for t in range(4):
+            nc.tensor.transpose(ub_ps[:, cols(t)], ucol[:, t : t + 1].to_broadcast([P, P]), ident[:])
+
+        rt = [bank(t) for t in range(RT)]
+        for h in range(2):
+            for t in range(RT):
+                first_product(rt[t], w2w, w2s, t, slice(HALF * h, HALF * (h + 1)))
+
+        ub = keep.tile([P, H], F32, name="ub")
+        nc.vector.tensor_scalar(ub[:].rearrange("j (p t) -> j p t", t=4), ub_ps[:].rearrange("j (t p) -> j p t", t=4), 0.3, None, ALU.mult)
+
+        ra = wide("ra")
+        for h in range(2):
+            nc.scalar.activation(ra[:, 2 * h : 2 * h + 2, :], a_t[:, 2 * h : 2 * h + 2, :], ACT.Abs_reciprocal_sqrt, scale=25.0)
+
+        neg = wide("neg")
+        d = wide("d")
+        th = wide("th")
+        y = wide("y")
+        k = wide("k")
+        c0 = wide("c0")
+        vg = wide("vg")
+
+        for t in range(RT):
+            if t % 2 == 0:
+                nc.scalar.activation(win[t][:, 0:S], rt[t][:], ACT.Copy, bias=0.2)
+            else:
+                nc.vector.tensor_scalar(win[t][:, 0:S], rt[t][:], 0.2, None, ALU.add)
+            nc.vector.tensor_scalar(neg[:, t, :], win[t][:, 0:S], -1.0, None, ALU.mult)
+            nc.vector.tensor_tensor(d[:, t, :], win[t][:].indirect(shl_t[:]), neg[:, t, :], ALU.add)
+        po = []
+        for t in range(RT):
+            nc.scalar.activation(a_t[:, :, cols(t)], rt[t][:].rearrange("p (b j) -> p b j", b=NB), ACT.Sigmoid, scale=-1.0)
+            po.append(bank(t))
+            first_product(po[t], w1w, w1s, t, slice(0, S))
+        for t in range(RT):
+            nc.scalar.activation(th[:, t, :], po[t][:], ACT.Tanh, scale=0.5)
+            nc.vector.scalar_tensor_tensor(y[:, t, :], th[:, t, :], 1.25, ra[:, t, :], ALU.add, ALU.mult)
+        for t in range(RT):
+            nc.scalar.activation(vb[t][:, 0:S], d[:, t, :], ACT.Sigmoid, scale=-1.0)
+            nc.scalar.activation(k[:, t, :], y[:, t, :], ACT.Square)
+            nc.vector.scalar_tensor_tensor(c0[:, t, :], k[:, t, :], -0.5, vb[t][:, 0:S], ALU.add, ALU.mult)
+
+
+        nr = wide("nr")
+        ncr = wide("ncr")
+        e0 = wide("e0")
+        lnd = wide("lnd")
+        lne = wide("lne")
+        diff = wide("diff")
+        hh = wide("hh")
+
+        def row(buf, b):
+            return buf[:, b, :].rearrange("p (t j) -> p t j", t=RT)
+
+        for b in range(NB):
+            nc.scalar.activation(d[:, :, cols(b)], row(a_t, b), ACT.Ln, scale=math.exp(-0.2), bias=TINY)
+        for b in range(NB):
+            nc.vector.tensor_tensor(row(nr, b), d[:, :, cols(b)], neg[:, :, cols(b)], ALU.min)
+            nc.vector.scalar_tensor_tensor(row(ncr, b), c0[:, :, cols(b)], 0.5, row(nr, b), ALU.add, ALU.mult)
+            nc.vector.scalar_tensor_tensor(row(e0, b), row(ncr, b), -0.02, c0[:, :, cols(b)], ALU.mult, ALU.add)
+            nc.scalar.activation(lnd[:, b, :], ncr[:, b, :], ACT.Ln, scale=-1.0, bias=0.1)
+            nc.scalar.activation(lne[:, b, :], e0[:, b, :], ACT.Ln, bias=0.502)
+        for b in range(NB):
+            nc.vector.tensor_tensor(diff[:, b, :], lne[:, b, :], lnd[:, b, :], ALU.subtract)
+
+        for t in range(RT):
+            if t >= ON_VECTOR:
+                nc.scalar.activation(vg[:, t, :], vb[t][:].indirect(shl_t[:]), ACT.Copy)
+            else:
+                nc.vector.tensor_copy(vg[:, t, :], vb[t][:].indirect(shl_t[:]))
+        xt = [bank(b) for b in range(NB)]
+        for t in range(RT):
+            for b in range(NB):
+                nc.tensor.matmul(xt[b][:, cols(t)], lhsT=vg[:, t, cols(b)], rhs=ident[:], is_transpose=True, start=(t == 0), stop=False)
+
+        out_v = out.rearrange("(m p) j -> p m j", p=P)
+        for b in range(NB):
+            nc.scalar.activation(e0[:, :, cols(b)], row(diff, b), ACT.Exp, scale=0.5, bias=math.log(2.0 / 3.0))
+        for b in range(NB):
+            nc.vector.scalar_tensor_tensor(row(hh, b), th[:, :, cols(b)], 1.25, e0[:, :, cols(b)], ALU.add, ALU.mult)
+            for t in range(RT):
+                nc.tensor.matmul(xt[b][:, cols(t)], lhsT=hh[:, b, cols(t)], rhs=ident[:], is_transpose=True, start=False, stop=(t == RT - 1))
+        for b in range(NB):
+            hid_t = keep.tile([P, H], BF16, name="hid_t%d" % b, align_bytes=64)
+            nc.vector.scalar_tensor_tensor(hid_t[:], xt[b][:], -1.0, ub[:], ALU.add, ALU.mult)
+            words = hid_t[:].bitcast(F32)
+            turned = bank(4 + b % 2)
+            for u in range(2):
+                nc.tensor.transpose(turned[:, cols(u)], words[:, u : H // 2 : 2], ident[:])
+            grouped = keep.tile([P, 4 * P], BF16, name="grouped%d" % b, align_bytes=64)
+            nc.scalar.copy(grouped[:].bitcast(F32).rearrange("p (j u) -> p j u", u=2), turned[:, 0 : 2 * P].rearrange("p (u j) -> p j u", u=2))
+            codes = keep.tile([P, P], U32, name="codes%d" % b, align_bytes=64)
+            plane = keep.tile([P, P], U8, name="plane%d" % b, align_bytes=64)
+            nc.vector.quantize_mx(out=codes[:].bitcast(FP8X4), scales=plane[:], in_=grouped[:])
+            acc = bank(6 + b % 2)
+            for m in range(MT):
+                nc.tensor.matmul_mx(
+                    out=acc[:, cols(m)],
+                    lhsT=w3w[:, 2 * P * m : 2 * P * (m + 1)].bitcast(FP4X4),
+                    lhsT_scale=w3s[:, cols(m)],
+                    rhs=codes[:].bitcast(FP8X4),
+                    rhs_scale=plane[:],
+                    start=True,
+                    stop=True,
+                )
+            res = keep.tile([P, MT, P], F32, name="res%d" % b)
+            nc.scalar.copy(res[:], acc[:, 0 : MT * P].rearrange("p (m j) -> p m j", m=MT))
+            nc.sync.dma_start(out=out_v[:, :, cols(b)], in_=res[:])

@@ -24,7 +24,7 @@ NB = S // P
 MT = N // P
 HALF = S // 2
 TINY = 1e-14
-ON_VECTOR = 2
+ON_SCALAR = (1,)
 
 
 def load_scales(nc, plane, scales):
@@ -53,44 +53,39 @@ def tile_picked_yarchi_bvw_p_kernel(tc, x_words, x_scales, w1_words, w1_scales, 
         xs = keep.tile([P, T], U8, name="xs", align_bytes=64)
         w2w = keep.tile([P, 2 * H], U8, name="w2w", align_bytes=64)
         w1w = keep.tile([P, 2 * H], U8, name="w1w", align_bytes=64)
-        w3w = keep.tile([P, 2 * N], U8, name="w3w", align_bytes=64)
         w2s = keep.tile([P, H], U8, name="w2s", align_bytes=64)
         w1s = keep.tile([P, H], U8, name="w1s", align_bytes=64)
-        w3s = keep.tile([P, N], U8, name="w3s", align_bytes=64)
         ucol = keep.tile([P, 4], F32, name="ucol")
         ident = keep.tile([P, P], F32, name="ident")
         a_t = wide("a_t")
 
-        for plane in (xs, w2s):
+        for plane in (xs, w2s, w1s):
             nc.vector.memset(plane[:].bitcast(I32), 0)
-        for plane in (w1s, w3s):
-            nc.vector.memset(plane[:].bitcast(I32), 0)
-        win = [keep.tile([P, S + 16], F32, name="win%d" % t, align_bytes=64) for t in range(RT)]
-        vb = [keep.tile([P, S + (192 if t < ON_VECTOR else 16)], F32, name="vb%d" % t, align_bytes=64) for t in range(RT)]
-        for window in win + vb:
+        win = [keep.tile([P, S], F32, name="win%d" % t, align_bytes=64) for t in range(RT)]
+        vb = [keep.tile([P, S + (16 if t in ON_SCALAR else 192)], F32, name="vb%d" % t, align_bytes=64) for t in range(RT)]
+        for window in vb:
             nc.vector.memset(window[:, S:], 0.0)
 
         a_v = aa.rearrange("(t p) j -> p t j", p=P)
+        nc.sync.dma_start(out=xw[:], in_=x_words[0].rearrange("p n t -> p (n t)").bitcast(I32))
         nc.sync.dma_start(offs_t[:], offs)
         load_scales(nc, xs, x_scales)
-        nc.sync.dma_start(out=xw[:], in_=x_words[0].rearrange("p n t -> p (n t)").bitcast(I32))
-        nc.sync.dma_start(out=a_t[:, 0:2, :], in_=a_v[:, 0:2, :])
-        nc.sync.dma_start(out=a_t[:, 2:4, :], in_=a_v[:, 2:4, :])
-        load_scales(nc, w2s, w2_scales)
         nc.sync.dma_start(out=w2w[:].bitcast(I32), in_=w2_words[0].bitcast(I32))
+        nc.sync.dma_start(out=a_t[:, 0:2, :], in_=a_v[:, 0:2, :])
+        load_scales(nc, w2s, w2_scales)
+        nc.sync.dma_start(out=a_t[:, 2:4, :], in_=a_v[:, 2:4, :])
         nc.sync.dma_start(shl_t[:], shl)
         nc.sync.dma_start(out=w1w[:].bitcast(I32), in_=w1_words[0].bitcast(I32))
         load_scales(nc, w1s, w1_scales)
-        nc.gpsimd.dma_start(out=ucol[:], in_=unit.rearrange("(p t) o -> p (t o)", t=4))
-        nc.sync.dma_start(out=w3w[:].bitcast(I32), in_=w3_words[0].bitcast(I32))
-        load_scales(nc, w3s, w3_scales)
+        nc.sync.dma_start(out=ucol[:], in_=unit.rearrange("(p t) o -> p (t o)", t=4))
         make_identity(nc, ident[:])
 
         xg = keep.tile([P, S], U32, name="xg", align_bytes=64)
         xsg = keep.tile([P, S], U8, name="xsg", align_bytes=64)
-        nc.vector.tensor_copy(xsg[:], xs[:].indirect(offs_t[:]))
         for h in range(2):
-            nc.vector.tensor_copy(xg[:, HALF * h : HALF * (h + 1)], xw[:].bitcast(U32).indirect(offs_t[:, (HALF // 16) * h : (HALF // 16) * (h + 1)]))
+            places = offs_t[:, (HALF // 16) * h : (HALF // 16) * (h + 1)]
+            nc.vector.tensor_copy(xg[:, HALF * h : HALF * (h + 1)], xw[:].bitcast(U32).indirect(places))
+            nc.vector.tensor_copy(xsg[:, HALF * h : HALF * (h + 1)], xs[:].indirect(places))
 
         def first_product(acc, words, plane, t, js):
             nc.tensor.matmul_mx(
@@ -103,17 +98,10 @@ def tile_picked_yarchi_bvw_p_kernel(tc, x_words, x_scales, w1_words, w1_scales, 
                 stop=True,
             )
 
-        ub_ps = bank(4)
-        for t in range(4):
-            nc.tensor.transpose(ub_ps[:, cols(t)], ucol[:, t : t + 1].to_broadcast([P, P]), ident[:])
-
         rt = [bank(t) for t in range(RT)]
-        for h in range(2):
-            for t in range(RT):
+        for t in range(RT):
+            for h in range(2):
                 first_product(rt[t], w2w, w2s, t, slice(HALF * h, HALF * (h + 1)))
-
-        ub = keep.tile([P, H], F32, name="ub")
-        nc.vector.tensor_scalar(ub[:].rearrange("j (p t) -> j p t", t=4), ub_ps[:].rearrange("j (t p) -> j p t", t=4), 0.3, None, ALU.mult)
 
         ra = wide("ra")
         for h in range(2):
@@ -125,32 +113,44 @@ def tile_picked_yarchi_bvw_p_kernel(tc, x_words, x_scales, w1_words, w1_scales, 
         y = wide("y")
         k = wide("k")
         c0 = wide("c0")
-        vg = wide("vg")
+        vg = [y[:, RT - 1, :], k[:, RT - 1, :], k[:, RT - 2, :], c0[:, RT - 1, :]]
 
         for t in range(RT):
-            if t % 2 == 0:
-                nc.scalar.activation(win[t][:, 0:S], rt[t][:], ACT.Copy, bias=0.2)
+            nc.vector.tensor_scalar(win[t][:, 0:S], rt[t][:], 0.2, 0.02, ALU.add, ALU.mult)
+            if t == 0:
+                nc.vector.tensor_copy(neg[:, t, :], win[t][:, 0:S])
             else:
-                nc.vector.tensor_scalar(win[t][:, 0:S], rt[t][:], 0.2, None, ALU.add)
-            nc.vector.tensor_scalar(neg[:, t, :], win[t][:, 0:S], -1.0, None, ALU.mult)
-            nc.vector.tensor_tensor(d[:, t, :], win[t][:].indirect(shl_t[:]), neg[:, t, :], ALU.add)
+                nc.sync.dma_start(out=neg[:, t, :], in_=win[t][:, 0:S])
+        for t in range(RT):
+            for h in range(2):
+                js = slice(HALF * h, HALF * (h + 1))
+                nc.vector.tensor_tensor(d[:, t, js], win[t][:].indirect(shl_t[:, (HALF // 16) * h : (HALF // 16) * (h + 1)]), neg[:, t, js], ALU.subtract)
         po = []
         for t in range(RT):
             nc.scalar.activation(a_t[:, :, cols(t)], rt[t][:].rearrange("p (b j) -> p b j", b=NB), ACT.Sigmoid, scale=-1.0)
             po.append(bank(t))
             first_product(po[t], w1w, w1s, t, slice(0, S))
+        w3w = w1w[:, 0 : 2 * N]
+        w3s = w1s[:, 0:N]
+        nc.sync.dma_start(out=w3w.bitcast(I32), in_=w3_words[0].bitcast(I32))
+        load_scales(nc, w3s, w3_scales)
         for t in range(RT):
             nc.scalar.activation(th[:, t, :], po[t][:], ACT.Tanh, scale=0.5)
             nc.vector.scalar_tensor_tensor(y[:, t, :], th[:, t, :], 1.25, ra[:, t, :], ALU.add, ALU.mult)
+        esum = [bank(4 + b) for b in range(NB)]
         for t in range(RT):
-            nc.scalar.activation(vb[t][:, 0:S], d[:, t, :], ACT.Sigmoid, scale=-1.0)
-            nc.scalar.activation(k[:, t, :], y[:, t, :], ACT.Square)
+            nc.scalar.activation(vb[t][:, 0:S], d[:, t, :], ACT.Sigmoid, scale=-50.0)
+            if t == 0:
+                nc.vector.tensor_tensor(k[:, t, :], y[:, t, :], y[:, t, :], ALU.mult)
+            else:
+                nc.scalar.activation(k[:, t, :], y[:, t, :], ACT.Square)
             nc.vector.scalar_tensor_tensor(c0[:, t, :], k[:, t, :], -0.5, vb[t][:, 0:S], ALU.add, ALU.mult)
+            for b in range(NB):
+                nc.tensor.matmul(esum[b][:, cols(t)], lhsT=c0[:, t, cols(b)], rhs=ident[:], is_transpose=True, start=(t == 0), stop=False)
 
 
         nr = wide("nr")
         ncr = wide("ncr")
-        e0 = wide("e0")
         lnd = wide("lnd")
         lne = wide("lne")
         diff = wide("diff")
@@ -162,38 +162,54 @@ def tile_picked_yarchi_bvw_p_kernel(tc, x_words, x_scales, w1_words, w1_scales, 
         for b in range(NB):
             nc.scalar.activation(d[:, :, cols(b)], row(a_t, b), ACT.Ln, scale=math.exp(-0.2), bias=TINY)
         for b in range(NB):
-            nc.vector.tensor_tensor(row(nr, b), d[:, :, cols(b)], neg[:, :, cols(b)], ALU.min)
+            nc.vector.scalar_tensor_tensor(row(nr, b), d[:, :, cols(b)], -0.02, neg[:, :, cols(b)], ALU.mult, ALU.max)
             nc.vector.scalar_tensor_tensor(row(ncr, b), c0[:, :, cols(b)], 0.5, row(nr, b), ALU.add, ALU.mult)
-            nc.vector.scalar_tensor_tensor(row(e0, b), row(ncr, b), -0.02, c0[:, :, cols(b)], ALU.mult, ALU.add)
-            nc.scalar.activation(lnd[:, b, :], ncr[:, b, :], ACT.Ln, scale=-1.0, bias=0.1)
-            nc.scalar.activation(lne[:, b, :], e0[:, b, :], ACT.Ln, bias=0.502)
+            for t in range(RT):
+                nc.tensor.matmul(esum[b][:, cols(t)], lhsT=ncr[:, b, cols(t)], rhs=ident[:], is_transpose=True, start=False, stop=(t == RT - 1))
+            nc.scalar.activation(lnd[:, b, :], ncr[:, b, :], ACT.Ln, scale=50.0, bias=0.1)
+            nc.scalar.activation(lne[:, b, :], esum[b][:], ACT.Ln, bias=0.502)
         for b in range(NB):
-            nc.vector.tensor_tensor(diff[:, b, :], lne[:, b, :], lnd[:, b, :], ALU.subtract)
+            back = bank(4 + b)
+            for t in range(RT):
+                nc.tensor.transpose(back[:, cols(t)], lne[:, b, cols(t)], ident[:])
+            nc.vector.tensor_tensor(diff[:, b, :], back[:], lnd[:, b, :], ALU.subtract)
 
         for t in range(RT):
-            if t >= ON_VECTOR:
-                nc.scalar.activation(vg[:, t, :], vb[t][:].indirect(shl_t[:]), ACT.Copy)
+            if t in ON_SCALAR:
+                nc.scalar.activation(vg[t], vb[t][:].indirect(shl_t[:]), ACT.Copy)
             else:
-                nc.vector.tensor_copy(vg[:, t, :], vb[t][:].indirect(shl_t[:]))
+                nc.vector.tensor_copy(vg[t], vb[t][:].indirect(shl_t[:]))
         xt = [bank(b) for b in range(NB)]
         for t in range(RT):
             for b in range(NB):
-                nc.tensor.matmul(xt[b][:, cols(t)], lhsT=vg[:, t, cols(b)], rhs=ident[:], is_transpose=True, start=(t == 0), stop=False)
+                nc.tensor.matmul(xt[b][:, cols(t)], lhsT=vg[t][:, cols(b)], rhs=ident[:], is_transpose=True, start=(t == 0), stop=False)
 
         out_v = out.rearrange("(m p) j -> p m j", p=P)
         for b in range(NB):
-            nc.scalar.activation(e0[:, :, cols(b)], row(diff, b), ACT.Exp, scale=0.5, bias=math.log(2.0 / 3.0))
+            nc.scalar.activation(lne[:, :, cols(b)], row(diff, b), ACT.Exp, scale=0.5, bias=math.log(2.0 / 3.0))
+        ub_ps = bank(7)
+        for t in range(4):
+            nc.tensor.transpose(ub_ps[:, cols(t)], ucol[:, t : t + 1].to_broadcast([P, P]), ident[:])
+        ub = keep.tile([P, H], F32, name="ub")
+        nc.scalar.activation(ub[:].rearrange("j (u p e) -> j u p e", u=2, e=2), ub_ps[:].rearrange("j (u e p) -> j u p e", u=2, e=2), ACT.Copy, scale=0.3)
         for b in range(NB):
-            nc.vector.scalar_tensor_tensor(row(hh, b), th[:, :, cols(b)], 1.25, e0[:, :, cols(b)], ALU.add, ALU.mult)
+            nc.vector.scalar_tensor_tensor(row(hh, b), th[:, :, cols(b)], 1.25, lne[:, :, cols(b)], ALU.add, ALU.mult)
             for t in range(RT):
                 nc.tensor.matmul(xt[b][:, cols(t)], lhsT=hh[:, b, cols(t)], rhs=ident[:], is_transpose=True, start=False, stop=(t == RT - 1))
         for b in range(NB):
             hid_t = keep.tile([P, H], BF16, name="hid_t%d" % b, align_bytes=64)
-            nc.vector.scalar_tensor_tensor(hid_t[:], xt[b][:], -1.0, ub[:], ALU.add, ALU.mult)
-            words = hid_t[:].bitcast(F32)
             turned = bank(4 + b % 2)
             for u in range(2):
-                nc.tensor.transpose(turned[:, cols(u)], words[:, u : H // 2 : 2], ident[:])
+                part = slice(2 * P * u, 2 * P * (u + 1))
+                nc.vector.scalar_tensor_tensor(
+                    hid_t[:, part].rearrange("j (p e) -> j p e", e=2),
+                    xt[b][:].rearrange("j (p t) -> j p t", t=4)[:, :, 2 * u : 2 * u + 2],
+                    -1.0,
+                    ub[:, part].rearrange("j (p e) -> j p e", e=2),
+                    ALU.add,
+                    ALU.mult,
+                )
+                nc.tensor.transpose(turned[:, cols(u)], hid_t[:, part].bitcast(F32), ident[:])
             grouped = keep.tile([P, 4 * P], BF16, name="grouped%d" % b, align_bytes=64)
             nc.scalar.copy(grouped[:].bitcast(F32).rearrange("p (j u) -> p j u", u=2), turned[:, 0 : 2 * P].rearrange("p (u j) -> p j u", u=2))
             codes = keep.tile([P, P], U32, name="codes%d" % b, align_bytes=64)

import math
from contextlib import ExitStack

import concourse.mybir as mybir
from concourse.masks import make_identity

K, T, S, N, H = 512, 1024, 512, 256, 512
FLOPS = 2 * K * S * H * 2 + 2 * H * S * N

F32 = mybir.dt.float32
BF16 = mybir.dt.bfloat16
I32 = mybir.dt.int32
U32 = mybir.dt.uint32
U16 = mybir.dt.uint16
U8 = mybir.dt.uint8
FP8X4 = mybir.dt.float8_e4m3fn_x4
FP4X4 = mybir.dt.float4_e2m1fn_x4
ACT = mybir.ActivationFunctionType
ALU = mybir.AluOpType

P = 128
RT = H // P
NB = S // P
MT = N // P
HALF = S // 2
TINY = 1e-14
ON_SCALAR = (1,)


def load_scales(nc, plane, scales):
    for q in range(4):
        nc.sync.dma_start(out=plane[32 * q : 32 * q + 4, :].bitcast(I32), in_=scales[0, 4 * q : 4 * q + 4, :].bitcast(I32))


def tile_picked_yarchi_bvw_p_kernel(tc, x_words, x_scales, w1_words, w1_scales, w2_words, w2_scales, aa, unit, w3_words, w3_scales, offs, shl, out):
    nc = tc.nc
    with ExitStack() as ctx:
        keep = ctx.enter_context(tc.tile_pool(name="keep", bufs=1))
        psum = ctx.enter_context(tc.psum_pool(name="psum", bufs=1))

        def bank(n):
            return psum.tile([P, S], F32, name="bank%d" % n)

        def wide(name):
            return keep.tile([P, RT, S], F32, name=name, align_bytes=64)

        def cols(b):
            return slice(P * b, P * (b + 1))

        offs_t = keep.tile([P, S // 16], U16, name="offs_t")
        shl_t = keep.tile([P, S // 16], U16, name="shl_t")
        xw = keep.tile([P, T], I32, name="xw", align_bytes=64)
        xs = keep.tile([P, T], U8, name="xs", align_bytes=64)
        w2w = keep.tile([P, 2 * H], U8, name="w2w", align_bytes=64)
        w1w = keep.tile([P, 2 * H], U8, name="w1w", align_bytes=64)
        w2s = keep.tile([P, H], U8, name="w2s", align_bytes=64)
        w1s = keep.tile([P, H], U8, name="w1s", align_bytes=64)
        ucol = keep.tile([P, 4], F32, name="ucol")
        ident = keep.tile([P, P], F32, name="ident")
        a_t = wide("a_t")

        for plane in (xs, w2s, w1s):
            nc.vector.memset(plane[:].bitcast(I32), 0)
        win = [keep.tile([P, S], F32, name="win%d" % t, align_bytes=64) for t in range(RT)]
        vb = [keep.tile([P, S + (16 if t in ON_SCALAR else 192)], F32, name="vb%d" % t, align_bytes=64) for t in range(RT)]
        for window in vb:
            nc.vector.memset(window[:, S:], 0.0)

        a_v = aa.rearrange("(t p) j -> p t j", p=P)
        nc.sync.dma_start(out=xw[:], in_=x_words[0].rearrange("p n t -> p (n t)").bitcast(I32))
        nc.sync.dma_start(offs_t[:], offs)
        load_scales(nc, xs, x_scales)
        nc.sync.dma_start(out=w2w[:].bitcast(I32), in_=w2_words[0].bitcast(I32))
        nc.sync.dma_start(out=a_t[:, 0:2, :], in_=a_v[:, 0:2, :])
        load_scales(nc, w2s, w2_scales)
        nc.sync.dma_start(out=a_t[:, 2:4, :], in_=a_v[:, 2:4, :])
        nc.sync.dma_start(shl_t[:], shl)
        nc.sync.dma_start(out=w1w[:].bitcast(I32), in_=w1_words[0].bitcast(I32))
        load_scales(nc, w1s, w1_scales)
        nc.sync.dma_start(out=ucol[:], in_=unit.rearrange("(p t) o -> p (t o)", t=4))
        make_identity(nc, ident[:])

        xg = keep.tile([P, S], U32, name="xg", align_bytes=64)
        xsg = keep.tile([P, S], U8, name="xsg", align_bytes=64)
        for h in range(2):
            places = offs_t[:, (HALF // 16) * h : (HALF // 16) * (h + 1)]
            nc.vector.tensor_copy(xg[:, HALF * h : HALF * (h + 1)], xw[:].bitcast(U32).indirect(places))
            nc.vector.tensor_copy(xsg[:, HALF * h : HALF * (h + 1)], xs[:].indirect(places))

        def first_product(acc, words, plane, t, js):
            nc.tensor.matmul_mx(
                out=acc[:, js],
                lhsT=words[:, 2 * P * t : 2 * P * (t + 1)].bitcast(FP4X4),
                lhsT_scale=plane[:, cols(t)],
                rhs=xg[:, js].bitcast(FP8X4),
                rhs_scale=xsg[:, js],
                start=True,
                stop=True,
            )

        rt = [bank(t) for t in range(RT)]
        for t in range(RT):
            for h in range(2):
                first_product(rt[t], w2w, w2s, t, slice(HALF * h, HALF * (h + 1)))

        ra = wide("ra")
        for h in range(2):
            nc.scalar.activation(ra[:, 2 * h : 2 * h + 2, :], a_t[:, 2 * h : 2 * h + 2, :], ACT.Abs_reciprocal_sqrt, scale=25.0)

        neg = wide("neg")
        d = wide("d")
        th = wide("th")
        y = wide("y")
        k = wide("k")
        c0 = wide("c0")
        vg = [y[:, RT - 1, :], k[:, RT - 1, :], k[:, RT - 2, :], c0[:, RT - 1, :]]

        for t in range(RT):
            nc.vector.tensor_scalar(win[t][:, 0:S], rt[t][:], 0.2, 0.02, ALU.add, ALU.mult)
            if t == 0:
                nc.vector.tensor_copy(neg[:, t, :], win[t][:, 0:S])
            else:
                nc.sync.dma_start(out=neg[:, t, :], in_=win[t][:, 0:S])
        for t in range(RT):
            for h in range(2):
                js = slice(HALF * h, HALF * (h + 1))
                nc.vector.tensor_tensor(d[:, t, js], win[t][:].indirect(shl_t[:, (HALF // 16) * h : (HALF // 16) * (h + 1)]), neg[:, t, js], ALU.subtract)
        po = []
        for t in range(RT):
            nc.scalar.activation(a_t[:, :, cols(t)], rt[t][:].rearrange("p (b j) -> p b j", b=NB), ACT.Sigmoid, scale=-1.0)
            po.append(bank(t))
            first_product(po[t], w1w, w1s, t, slice(0, S))
        w3w = w1w[:, 0 : 2 * N]
        w3s = w1s[:, 0:N]
        nc.sync.dma_start(out=w3w.bitcast(I32), in_=w3_words[0].bitcast(I32))
        load_scales(nc, w3s, w3_scales)
        for t in range(RT):
            nc.scalar.activation(th[:, t, :], po[t][:], ACT.Tanh, scale=0.5)
            nc.vector.scalar_tensor_tensor(y[:, t, :], th[:, t, :], 1.25, ra[:, t, :], ALU.add, ALU.mult)
        esum = [bank(4 + b) for b in range(NB)]
        for t in range(RT):
            nc.scalar.activation(vb[t][:, 0:S], d[:, t, :], ACT.Sigmoid, scale=-50.0)
            if t == 0:
                nc.vector.tensor_tensor(k[:, t, :], y[:, t, :], y[:, t, :], ALU.mult)
            else:
                nc.scalar.activation(k[:, t, :], y[:, t, :], ACT.Square)
            nc.vector.scalar_tensor_tensor(c0[:, t, :], k[:, t, :], -0.5, vb[t][:, 0:S], ALU.add, ALU.mult)
            for b in range(NB):
                nc.tensor.matmul(esum[b][:, cols(t)], lhsT=c0[:, t, cols(b)], rhs=ident[:], is_transpose=True, start=(t == 0), stop=False)


        nr = wide("nr")
        ncr = wide("ncr")
        lnd = wide("lnd")
        lne = wide("lne")
        diff = wide("diff")
        hh = wide("hh")

        def row(buf, b):
            return buf[:, b, :].rearrange("p (t j) -> p t j", t=RT)

        for b in range(NB):
            nc.scalar.activation(d[:, :, cols(b)], row(a_t, b), ACT.Ln, scale=math.exp(-0.2), bias=TINY)
        for b in range(NB):
            nc.vector.scalar_tensor_tensor(row(nr, b), d[:, :, cols(b)], -0.02, neg[:, :, cols(b)], ALU.mult, ALU.max)
            nc.vector.scalar_tensor_tensor(row(ncr, b), c0[:, :, cols(b)], 0.5, row(nr, b), ALU.add, ALU.mult)
            for t in range(RT):
                nc.tensor.matmul(esum[b][:, cols(t)], lhsT=ncr[:, b, cols(t)], rhs=ident[:], is_transpose=True, start=False, stop=(t == RT - 1))
            nc.scalar.activation(lnd[:, b, :], ncr[:, b, :], ACT.Ln, scale=50.0, bias=0.1)
            nc.scalar.activation(lne[:, b, :], esum[b][:], ACT.Ln, bias=0.502)
        for b in range(NB):
            back = bank(4 + b)
            for t in range(RT):
                nc.tensor.transpose(back[:, cols(t)], lne[:, b, cols(t)], ident[:])
            nc.vector.tensor_tensor(diff[:, b, :], back[:], lnd[:, b, :], ALU.subtract)

        for t in range(RT):
            if t in ON_SCALAR:
                nc.scalar.activation(vg[t], vb[t][:].indirect(shl_t[:]), ACT.Copy)
            else:
                nc.vector.tensor_copy(vg[t], vb[t][:].indirect(shl_t[:]))
        xt = [bank(b) for b in range(NB)]
        for t in range(RT):
            for b in range(NB):
                nc.tensor.matmul(xt[b][:, cols(t)], lhsT=vg[t][:, cols(b)], rhs=ident[:], is_transpose=True, start=(t == 0), stop=False)

        out_v = out.rearrange("(m p) j -> p m j", p=P)
        for b in range(NB):
            nc.scalar.activation(lne[:, :, cols(b)], row(diff, b), ACT.Exp, scale=0.5, bias=math.log(2.0 / 3.0))
        ub_ps = bank(7)
        for t in range(4):
            nc.tensor.transpose(ub_ps[:, cols(t)], ucol[:, t : t + 1].to_broadcast([P, P]), ident[:])
        ub = keep.tile([P, H], F32, name="ub")
        nc.scalar.activation(ub[:].rearrange("j (u p e) -> j u p e", u=2, e=2), ub_ps[:].rearrange("j (u e p) -> j u p e", u=2, e=2), ACT.Copy, scale=0.3)
        for b in range(NB):
            nc.vector.scalar_tensor_tensor(row(hh, b), th[:, :, cols(b)], 1.25, lne[:, :, cols(b)], ALU.add, ALU.mult)
            for t in range(RT):
                nc.tensor.matmul(xt[b][:, cols(t)], lhsT=hh[:, b, cols(t)], rhs=ident[:], is_transpose=True, start=False, stop=(t == RT - 1))
        for b in range(NB):
            hid_t = keep.tile([P, H], BF16, name="hid_t%d" % b, align_bytes=64)
            turned = bank(4 + b % 2)
            for u in range(2):
                part = slice(2 * P * u, 2 * P * (u + 1))
                nc.vector.scalar_tensor_tensor(
                    hid_t[:, part].rearrange("j (p e) -> j p e", e=2),
                    xt[b][:].rearrange("j (p t) -> j p t", t=4)[:, :, 2 * u : 2 * u + 2],
                    -1.0,
                    ub[:, part].rearrange("j (p e) -> j p e", e=2),
                    ALU.add,
                    ALU.mult,
                )
                nc.tensor.transpose(turned[:, cols(u)], hid_t[:, part].bitcast(F32), ident[:])
            grouped = keep.tile([P, 4 * P], BF16, name="grouped%d" % b, align_bytes=64)
            nc.scalar.copy(grouped[:].bitcast(F32).rearrange("p (j u) -> p j u", u=2), turned[:, 0 : 2 * P].rearrange("p (u j) -> p j u", u=2))
            codes = keep.tile([P, P], U32, name="codes%d" % b, align_bytes=64)
            plane = keep.tile([P, P], U8, name="plane%d" % b, align_bytes=64)
            nc.vector.quantize_mx(out=codes[:].bitcast(FP8X4), scales=plane[:], in_=grouped[:])
            acc = bank(6 + b % 2)
            for m in range(MT):
                nc.tensor.matmul_mx(
                    out=acc[:, cols(m)],
                    lhsT=w3w[:, 2 * P * m : 2 * P * (m + 1)].bitcast(FP4X4),
                    lhsT_scale=w3s[:, cols(m)],
                    rhs=codes[:].bitcast(FP8X4),
                    rhs_scale=plane[:],
                    start=True,
                    stop=True,
                )
            res = keep.tile([P, MT, P], F32, name="res%d" % b)
            nc.scalar.copy(res[:], acc[:, 0 : MT * P].rearrange("p (m j) -> p m j", m=MT))
            nc.sync.dma_start(out=out_v[:, :, cols(b)], in_=res[:])
